import numpy as np
import ml_dtypes


def mxq(x, axis, fmt="e4m3"):
    dtype, down = {"e4m3": (ml_dtypes.float8_e4m3fn, 7), "e5m2": (ml_dtypes.float8_e5m2, 14)}[fmt]
    v = np.moveaxis(np.asarray(x, np.float32).astype(ml_dtypes.bfloat16).astype(np.float64), axis, -1)
    blocks = v.reshape(v.shape[:-1] + (-1, 32))
    amax = np.abs(blocks).max(-1, keepdims=True)
    byte = np.maximum(np.where(amax > 0, np.frexp(amax)[1] - 1 + 127, 0) - down, 1)
    scale = np.exp2(byte - 127.0)
    codes = (blocks / scale).astype(np.float32).astype(dtype).astype(np.float64)
    return np.moveaxis((codes * scale).reshape(v.shape), -1, axis)


WIDE = False


def mx_kscale(k):
    if not WIDE:
        return np.ones(k)
    levels = np.array([10, -10, 5, -5, 0])
    if k % 512:
        return np.exp2(np.random.permutation(np.resize(levels, k // 32))).repeat(32)
    a = np.empty((k // 512, 16))
    for p in range(k // 512):
        a[p, :8] = np.random.permutation(np.resize(levels, 8))
        for g in range(8):
            far = levels[np.abs(levels - a[p, g]) >= 10]
            a[p, g + 8] = far[np.random.randint(len(far))]
    return np.exp2(a.ravel()).repeat(32)


def f64(x):
    return np.asarray(x).astype(np.float64)


def striped(idx):
    return np.tile(idx.reshape(-1, 16).T, (8, 1)).astype(np.uint16)


def unstriped(offs):
    return offs[:16].T.reshape(-1).astype(np.int64)


E2M1 = np.array([0.0, 0.5, 1.0, 1.5, 2.0, 3.0, 4.0, 6.0, -0.0, -0.5, -1.0, -1.5, -2.0, -3.0, -4.0, -6.0])


def pack_weight(w, fmt):
    k, n = w.shape
    w = f64(np.asarray(w, np.float32).astype(ml_dtypes.bfloat16)).reshape(k // 32, 32, n)
    amax = np.abs(w).max(1)
    if fmt == "e4m3":
        byte = np.frexp(amax)[1] - 1 + 127 - 7
    else:
        mant, ex = np.frexp(amax / 6.0)
        byte = np.where(mant > 0.5, ex, ex - 1) + 127
    byte = np.clip(np.where(amax > 0, byte, 1), 1, 254)
    scaled = (w * np.exp2(127.0 - byte)[:, None, :]).reshape(k, n).astype(np.float32)
    by_word = np.ascontiguousarray(scaled.reshape(k // 512, 128, 4, n).transpose(0, 1, 3, 2))
    if fmt == "e4m3":
        words = by_word.astype(ml_dtypes.float8_e4m3fn).view(np.uint8)
    else:
        c = by_word.astype(ml_dtypes.float4_e2m1fn).view(np.uint8) & 0xF
        words = (c[..., 0::2] | (c[..., 1::2] << 4)).reshape(k // 512, 128, 2 * n)
    return np.ascontiguousarray(words), np.ascontiguousarray(byte.astype(np.uint8).reshape(k // 512, 16, n))


def unpack_weight(words, scales, fmt):
    g, _, n = scales.shape
    words = np.ascontiguousarray(words).reshape(g, 128, n, -1)
    if fmt == "e4m3":
        vals = words.view(ml_dtypes.float8_e4m3fn).astype(np.float64)
    else:
        nib = np.empty((g, 128, n, 4), np.uint8)
        nib[..., 0::2] = words & 0xF
        nib[..., 1::2] = words >> 4
        vals = E2M1[nib]
    vals = vals * np.repeat(np.exp2(scales.astype(np.float64) - 127.0), 8, axis=1)[..., None]
    return vals.transpose(0, 1, 3, 2).reshape(g * 512, n)


def relu2(v):
    return np.maximum(v, 0.0) ** 2


K, T, E, C, H, N, HOT = 512, 640, 15, 128, 512, 256, 7
TOP = 3


def by_expert(wq, xq):
    return np.concatenate([wq[e].T @ xq[:, e * C:(e + 1) * C] for e in range(E)], axis=1)


def setup_inputs():
    n = np.random.standard_normal
    s = mx_kscale(K)
    u = mx_kscale(H)
    deal = np.repeat(np.arange(E), C).reshape(TOP, T)[:, np.random.permutation(T)]
    deal = np.take_along_axis(deal, np.argsort(np.random.rand(TOP, T), axis=0), axis=0)
    for _ in range(8):
        s_, t_ = np.random.permutation(T).reshape(2, -1); r = np.random.randint(TOP, size=T // 2); x, y = deal[r, s_].copy(), deal[r, t_].copy()
        ok = ~((deal[:, s_] == y).any(0) | (deal[:, t_] == x).any(0)); deal[r[ok], s_[ok]] = y[ok]; deal[r[ok], t_[ok]] = x[ok]
    order = np.lexsort((np.random.rand(TOP * T), deal.reshape(-1)))
    slot_token = order % T; pos = np.empty(TOP * T, np.int64); pos[order] = np.arange(TOP * T); pos = pos.reshape(TOP, T)
    g = np.random.uniform(0.5, 1.5, (TOP, T)); g = g / g.sum(0)
    x = pack_weight(n((K, T)) * s[:, None], "e4m3")
    w1h = [pack_weight(m, "e4m3") for m in n((HOT, K, H)) / np.sqrt(K) / s[None, :, None] * u]
    w2h = [pack_weight(m, "e4m3") for m in n((HOT, H, N)) / np.sqrt(H) / u[None, :, None] ** 2]
    w1c = [pack_weight(m, "e2m1") for m in n((E - HOT, K, H)) / np.sqrt(K) / s[None, :, None] * u]
    w2c = [pack_weight(m, "e2m1") for m in n((E - HOT, H, N)) / np.sqrt(H) / u[None, :, None] ** 2]
    return {
        "x_words": x[0],
        "x_scales": x[1],
        "w1h_words": np.stack([m[0] for m in w1h]),
        "w1h_scales": np.stack([m[1] for m in w1h]),
        "w2h_words": np.stack([m[0] for m in w2h]),
        "w2h_scales": np.stack([m[1] for m in w2h]),
        "w1c_words": np.stack([m[0] for m in w1c]),
        "w1c_scales": np.stack([m[1] for m in w1c]),
        "w2c_words": np.stack([m[0] for m in w2c]),
        "w2c_scales": np.stack([m[1] for m in w2c]),
        "gate": np.stack([np.tile(r, (128, 1)) for r in g]).astype(np.float32),
        "offs": striped(slot_token),
        "pos1": striped(pos[0]),
        "pos2": striped(pos[1]),
        "pos3": striped(pos[2]),
    }


def reference(x_words, x_scales, w1h_words, w1h_scales, w2h_words, w2h_scales, w1c_words, w1c_scales, w2c_words, w2c_scales, gate, offs, pos1, pos2, pos3):
    w1h = np.stack([unpack_weight(w1h_words[e], w1h_scales[e], "e4m3") for e in range(HOT)])
    w2h = np.stack([unpack_weight(w2h_words[e], w2h_scales[e], "e4m3") for e in range(HOT)])
    w1c = np.stack([unpack_weight(w1c_words[e], w1c_scales[e], "e2m1") for e in range(E - HOT)])
    w2c = np.stack([unpack_weight(w2c_words[e], w2c_scales[e], "e2m1") for e in range(E - HOT)])
    idx = unstriped(offs)
    xq = unpack_weight(x_words, x_scales, "e4m3")[:, idx]
    w1 = [*w1h, *w1c]
    w2 = [*w2h, *w2c]
    h = relu2(by_expert(w1, xq))
    y = by_expert(w2, mxq(h, 0, "e4m3"))
    out = sum(f64(gate[r, :1]) * y[:, unstriped(p)] for r, p in enumerate((pos1, pos2, pos3)))
    return out

@@ -1,0 +1,232 @@
+from contextlib import ExitStack
+
+import concourse.mybir as mybir
+from concourse.masks import make_identity
+
+K, T, E, C, H, N, HOT = 512, 640, 15, 128, 512, 256, 7
+TOP = 3
+SLOTS = E * C
+FLOPS = 2 * SLOTS * (K * H + H * N)
+
+F32 = mybir.dt.float32
+BF16 = mybir.dt.bfloat16
+I32 = mybir.dt.int32
+U32 = mybir.dt.uint32
+U16 = mybir.dt.uint16
+U8 = mybir.dt.uint8
+FP8X4 = mybir.dt.float8_e4m3fn_x4
+FP4X4 = mybir.dt.float4_e2m1fn_x4
+ACT = mybir.ActivationFunctionType
+ALU = mybir.AluOpType
+
+P = 128
+PACK = 4
+LIST_ROWS = 16
+
+UNITS = [(7, 8), (9, 10), (11, 12), (13, 14), (0, 1), (2, 3), (4, 5), (6,)]
+RELU_ON_SCALAR = (7, 8, 9, 13, 2)
+TAIL = [(0, 0, 640), (1, 0, 384), (1, 384, 640)]
+
+
+def tile_moe_hot_mlp_relu2_kernel(
+    tc, x_words, x_scales, w1h_words, w1h_scales, w2h_words, w2h_scales,
+    w1c_words, w1c_scales, w2c_words, w2c_scales, gate, offs, pos1, pos2, pos3, out,
+):
+    nc = tc.nc
+    with ExitStack() as ctx:
+        keep = ctx.enter_context(tc.tile_pool(name="keep", bufs=1))
+        ring = ctx.enter_context(tc.tile_pool(name="ring", bufs=4))
+        slot_ring = ctx.enter_context(tc.tile_pool(name="slot_ring", bufs=3))
+        psum = ctx.enter_context(tc.psum_pool(name="psum", bufs=3))
+        psum_y = ctx.enter_context(tc.psum_pool(name="psum_y", bufs=2))
+
+        offs_sb = keep.tile([P, SLOTS // LIST_ROWS], U16, name="offs_sb")
+        pos_sb = [keep.tile([P, T // LIST_ROWS], U16, name="pos_sb%d" % r) for r in range(TOP)]
+        x_win = keep.tile([P, T], I32, name="x_win", align_bytes=64)
+        xs_win = keep.tile([P, 1, T], U8, name="xs_win", align_bytes=64)
+        s1h = keep.tile([P, HOT, H], U8, name="s1h", align_bytes=64)
+        s2h = keep.tile([P, HOT, N], U8, name="s2h", align_bytes=64)
+        s1c = keep.tile([P, E - HOT, H], U8, name="s1c", align_bytes=64)
+        s2c = keep.tile([P, E - HOT, N], U8, name="s2c", align_bytes=64)
+        gate_sb = keep.tile([P, TOP, T], F32, name="gate_sb")
+        y = [keep.tile([P, SLOTS], F32, name="y%d" % half) for half in range(N // P)]
+
+        for plane in (xs_win, s1c, s2c, s1h, s2h):
+            nc.vector.memset(plane[:].bitcast(I32), 0)
+
+        def load_scales(plane, rows):
+            for q in (0, 2, 1, 3):
+                nc.sync.dma_start(out=plane[32 * q : 32 * q + 4, :, :].bitcast(I32), in_=rows[q].bitcast(I32))
+
+        def scale_rows(scales):
+            return scales.rearrange("e s (q r) n -> q r (e s) n", r=4)
+
+        w1 = {}
+        w2 = {}
+
+        def load_words(store, label, words_hot, words_cold, experts, queue):
+            first = experts[0]
+            if first < HOT:
+                src = words_hot.rearrange("e s p n d -> p (e s) (n d)")[:, first : first + len(experts), :]
+            else:
+                src = words_cold.rearrange("e s p n -> p (e s) n")[:, first - HOT : first - HOT + len(experts), :]
+            words = keep.tile([P, len(experts), src.shape[2]], U8, name="%s_%d" % (label, first), align_bytes=64)
+            queue.dma_start(out=words[:].bitcast(I32), in_=src.bitcast(I32))
+            for place, e in enumerate(experts):
+                store[e] = words[:, place, :]
+
+        nc.sync.dma_start(out=x_win[:], in_=x_words.rearrange("s p t d -> p (s t d)").bitcast(I32))
+        nc.sync.dma_start(offs_sb[:], offs)
+        load_words(w1, "w1", w1h_words, w1c_words, (7, 8), nc.sync)
+        load_scales(xs_win, x_scales.rearrange("s (q r) t -> q r s t", r=4))
+        load_scales(s1c, scale_rows(w1c_scales))
+        load_words(w1, "w1", w1h_words, w1c_words, (9, 10), nc.sync)
+        load_scales(s2c, scale_rows(w2c_scales))
+        load_words(w2, "w2", w2h_words, w2c_words, (7, 8, 9, 10), nc.sync)
+        load_words(w1, "w1", w1h_words, w1c_words, (11, 12, 13, 14), nc.sync)
+        load_words(w2, "w2", w2h_words, w2c_words, (11, 12, 13, 14), nc.sync)
+        load_scales(s1h, scale_rows(w1h_scales))
+        load_scales(s2h, scale_rows(w2h_scales))
+        load_words(w1, "w1", w1h_words, w1c_words, (0, 1), nc.sync)
+        load_words(w1, "w1", w1h_words, w1c_words, (2, 3), nc.sync)
+        load_words(w2, "w2", w2h_words, w2c_words, (0, 1, 2, 3), nc.sync)
+        load_words(w1, "w1", w1h_words, w1c_words, (4, 5, 6), nc.sync)
+        load_words(w2, "w2", w2h_words, w2c_words, (4, 5, 6), nc.sync)
+        for tile_r, pos in zip(pos_sb, (pos1, pos2, pos3)):
+            nc.sync.dma_start(tile_r[:], pos)
+        nc.sync.dma_start(out=gate_sb[:], in_=gate.rearrange("r p t -> p r t"))
+
+        ident_raw = keep.tile([P, P], F32, name="ident_raw")
+        make_identity(nc, ident_raw[:])
+        ident = keep.tile([P, P], F32, name="ident")
+        nc.scalar.activation(ident[:], ident_raw[:], ACT.Relu)
+
+        def fmt(e):
+            return FP8X4 if e < HOT else FP4X4
+
+        def slots_of(experts):
+            return slice(experts[0] * C, (experts[-1] + 1) * C)
+
+        x_slot, xs_slot = {}, {}
+
+        def gather_tokens(unit):
+            words = slot_ring.tile([P, 2 * C], U32, name="slot_words", align_bytes=64)
+            scale_bytes = slot_ring.tile([P, 2 * C], U8, name="slot_bytes", align_bytes=64)
+            pieces = [(e,) for e in unit] if unit == UNITS[0] else [unit]
+            for piece in pieces:
+                cols = slots_of(piece)
+                entries = offs_sb[:, cols.start // LIST_ROWS : cols.stop // LIST_ROWS]
+                local = slice(cols.start - unit[0] * C, cols.stop - unit[0] * C)
+                nc.vector.tensor_copy(words[:, local], x_win[:].bitcast(U32).indirect(entries))
+                nc.vector.tensor_copy(scale_bytes[:, local], xs_win[:, 0, :].indirect(entries))
+            for place, e in enumerate(unit):
+                x_slot[e] = words[:, place * C : (place + 1) * C]
+                xs_slot[e] = scale_bytes[:, place * C : (place + 1) * C]
+
+        pre, relu, turned, h_bf, h_words, h_scales, y_bank = {}, {}, {}, {}, {}, {}, {}
+
+        def first_layer(unit):
+            for e in unit:
+                pre[e] = psum.tile([P, H], F32, name="pre")
+                nc.tensor.matmul_mx(
+                    out=pre[e][:],
+                    lhsT=x_slot[e].bitcast(FP8X4),
+                    lhsT_scale=xs_slot[e],
+                    rhs=w1[e].bitcast(fmt(e)),
+                    rhs_scale=s1h[:, e, :] if e < HOT else s1c[:, e - HOT, :],
+                    start=True,
+                    stop=True,
+                )
+
+        def rectify(unit):
+            for e in unit:
+                relu[e] = ring.tile([P, PACK, P], F32, name="relu")
+                src = pre[e][:].rearrange("s (m t) -> s t m", t=PACK)
+                if e in RELU_ON_SCALAR:
+                    nc.scalar.activation(relu[e][:], src, ACT.Relu)
+                else:
+                    nc.vector.tensor_scalar(relu[e][:], src, 0.0, None, ALU.max)
+
+        def turn(unit):
+            for e in unit:
+                turned[e] = psum.tile([P, PACK, C], F32, name="turned")
+                for t in range(PACK):
+                    nc.tensor.transpose(turned[e][:, t, :], relu[e][:, t, :], ident[:])
+
+        def square(unit):
+            h_bf[unit] = ring.tile([P, 2, C, PACK], BF16, name="h_bf", align_bytes=64)
+            for place, e in enumerate(unit):
+                nc.scalar.activation(h_bf[unit][:, place, :, :], turned[e][:].rearrange("m t s -> m s t"), ACT.Square)
+
+        def quantise(unit):
+            width = len(unit) * C
+            h_words[unit] = ring.tile([P, 2 * C], U32, name="h_words", align_bytes=64)
+            h_scales[unit] = ring.tile([P, 2 * C], U8, name="h_scales", align_bytes=64)
+            nc.vector.quantize_mx(
+                out=h_words[unit][:, :width].bitcast(FP8X4),
+                scales=h_scales[unit][:, :width],
+                in_=h_bf[unit][:].rearrange("m e s t -> m (e s t)")[:, : width * PACK],
+            )
+
+        def second_layer(unit):
+            y_bank[unit] = psum_y.tile([P, N // P, 2 * C], F32, name="y_bank")
+            for half in range(N // P):
+                for place, e in enumerate(unit):
+                    word_bytes = 4 if e < HOT else 2
+                    cols = slice(place * C, (place + 1) * C)
+                    plane = s2h[:, e, :] if e < HOT else s2c[:, e - HOT, :]
+                    nc.tensor.matmul_mx(
+                        out=y_bank[unit][:, half, cols],
+                        lhsT=w2[e][:, half * P * word_bytes : (half + 1) * P * word_bytes].bitcast(fmt(e)),
+                        lhsT_scale=plane[:, half * P : (half + 1) * P],
+                        rhs=h_words[unit][:, cols].bitcast(FP8X4),
+                        rhs_scale=h_scales[unit][:, cols],
+                        start=True,
+                        stop=True,
+                    )
+
+        def keep_results(unit):
+            for half in range(N // P):
+                nc.scalar.copy(y[half][:, slots_of(unit)], y_bank[unit][:, half, : len(unit) * C])
+
+        def stage(work, index):
+            if 0 <= index < len(UNITS):
+                work(UNITS[index])
+
+        gather_tokens(UNITS[0])
+        gather_tokens(UNITS[1])
+        for j in range(-1, len(UNITS) + 2):
+            stage(first_layer, j + 1)
+            stage(second_layer, j - 2)
+            stage(square, j - 1)
+            stage(rectify, j + 1)
+            stage(keep_results, j - 2)
+            stage(gather_tokens, j + 3)
+            stage(quantise, j - 1)
+            stage(turn, j)
+
+        positions = pos_sb
+        terms = {}
+
+        def fetch(piece, r):
+            half, t0, t1 = piece
+            terms[piece, r] = keep.tile([P, t1 - t0], F32, name="term_%d_%d_%d" % (half, t0, r))
+            entries = positions[r][:, t0 // LIST_ROWS : t1 // LIST_ROWS]
+            nc.vector.tensor_tensor(terms[piece, r][:], y[half][:].indirect(entries), gate_sb[:, r, t0:t1], ALU.mult)
+
+        def add_first(piece):
+            nc.vector.tensor_tensor(terms[piece, 0][:], terms[piece, 0][:], terms[piece, 1][:], ALU.add)
+
+        def add_last(piece):
+            half, t0, t1 = piece
+            nc.vector.tensor_tensor(terms[piece, 0][:], terms[piece, 0][:], terms[piece, 2][:], ALU.add)
+            nc.sync.dma_start(out=out[half * P : (half + 1) * P, t0:t1], in_=terms[piece, 0][:])
+
+        for index, piece in enumerate(TAIL):
+            fetch(piece, 0)
+            if index > 0:
+                add_last(TAIL[index - 1])
+            fetch(piece, 1)
+            fetch(piece, 2)
+            add_first(piece)
+        add_last(TAIL[-1])

@@ -24,7 +24,8 @@ PACK = 4
 LIST_ROWS = 16
 
 UNITS = [(7, 8), (9, 10), (11, 12), (13, 14), (0, 1), (2, 3), (4, 5), (6,)]
-RELU_ON_SCALAR = (7, 8, 9, 13, 2)
+RELU_ON_SCALAR = (0, 1, 2, 7, 8, 9, 13, 14)
+KEEP_ON_VECTOR = ((7, 0), (7, 1), (9, 0), (9, 1), (11, 1), (13, 1), (0, 1), (4, 1))
 TAIL = [(0, 0, 640), (1, 0, 384), (1, 384, 640)]
 
 
@@ -37,6 +38,7 @@ def tile_moe_hot_mlp_relu2_kernel(
         keep = ctx.enter_context(tc.tile_pool(name="keep", bufs=1))
         ring = ctx.enter_context(tc.tile_pool(name="ring", bufs=4))
         slot_ring = ctx.enter_context(tc.tile_pool(name="slot_ring", bufs=3))
+        codes = ctx.enter_context(tc.tile_pool(name="codes", bufs=len(UNITS)))
         psum = ctx.enter_context(tc.psum_pool(name="psum", bufs=3))
         psum_y = ctx.enter_context(tc.psum_pool(name="psum_y", bufs=2))
 
@@ -54,9 +56,9 @@ def tile_moe_hot_mlp_relu2_kernel(
         for plane in (xs_win, s1c, s2c, s1h, s2h):
             nc.vector.memset(plane[:].bitcast(I32), 0)
 
-        def load_scales(plane, rows):
-            for q in (0, 2, 1, 3):
-                nc.sync.dma_start(out=plane[32 * q : 32 * q + 4, :, :].bitcast(I32), in_=rows[q].bitcast(I32))
+        def load_scales(plane, rows, queue=nc.sync, quadrants=(0, 2, 1, 3)):
+            for q in quadrants:
+                queue.dma_start(out=plane[32 * q : 32 * q + 4, :, :].bitcast(I32), in_=rows[q].bitcast(I32))
 
         def scale_rows(scales):
             return scales.rearrange("e s (q r) n -> q r (e s) n", r=4)
@@ -75,29 +77,27 @@ def tile_moe_hot_mlp_relu2_kernel(
             for place, e in enumerate(experts):
                 store[e] = words[:, place, :]
 
-        nc.sync.dma_start(out=x_win[:], in_=x_words.rearrange("s p t d -> p (s t d)").bitcast(I32))
+        ident_raw = keep.tile([P, P], F32, name="ident_raw")
+        x_rows = x_scales.rearrange("s (q r) t -> q r s t", r=4)
+        nc.scalar.dma_start(out=x_win[:], in_=x_words.rearrange("s p t d -> p (s t d)").bitcast(I32))
+        load_scales(xs_win, x_rows, nc.scalar, (1, 3))
+        load_words(w1, "w1", w1h_words, w1c_words, (7, 8, 9, 10), nc.gpsimd)
+        make_identity(nc, ident_raw[:])
+        load_words(w1, "w1", w1h_words, w1c_words, (11, 12, 13, 14), nc.gpsimd)
+        load_words(w2, "w2", w2h_words, w2c_words, tuple(range(HOT, E)), nc.gpsimd)
+        load_words(w1, "w1", w1h_words, w1c_words, (0, 1, 2, 3), nc.gpsimd)
+        load_words(w1, "w1", w1h_words, w1c_words, (4, 5, 6), nc.gpsimd)
+        load_words(w2, "w2", w2h_words, w2c_words, tuple(range(HOT)), nc.gpsimd)
         nc.sync.dma_start(offs_sb[:], offs)
-        load_words(w1, "w1", w1h_words, w1c_words, (7, 8), nc.sync)
-        load_scales(xs_win, x_scales.rearrange("s (q r) t -> q r s t", r=4))
+        load_scales(xs_win, x_rows, nc.sync, (0, 2))
         load_scales(s1c, scale_rows(w1c_scales))
-        load_words(w1, "w1", w1h_words, w1c_words, (9, 10), nc.sync)
-        load_scales(s2c, scale_rows(w2c_scales))
-        load_words(w2, "w2", w2h_words, w2c_words, (7, 8, 9, 10), nc.sync)
-        load_words(w1, "w1", w1h_words, w1c_words, (11, 12, 13, 14), nc.sync)
-        load_words(w2, "w2", w2h_words, w2c_words, (11, 12, 13, 14), nc.sync)
         load_scales(s1h, scale_rows(w1h_scales))
+        load_scales(s2c, scale_rows(w2c_scales))
         load_scales(s2h, scale_rows(w2h_scales))
-        load_words(w1, "w1", w1h_words, w1c_words, (0, 1), nc.sync)
-        load_words(w1, "w1", w1h_words, w1c_words, (2, 3), nc.sync)
-        load_words(w2, "w2", w2h_words, w2c_words, (0, 1, 2, 3), nc.sync)
-        load_words(w1, "w1", w1h_words, w1c_words, (4, 5, 6), nc.sync)
-        load_words(w2, "w2", w2h_words, w2c_words, (4, 5, 6), nc.sync)
         for tile_r, pos in zip(pos_sb, (pos1, pos2, pos3)):
             nc.sync.dma_start(tile_r[:], pos)
         nc.sync.dma_start(out=gate_sb[:], in_=gate.rearrange("r p t -> p r t"))
 
-        ident_raw = keep.tile([P, P], F32, name="ident_raw")
-        make_identity(nc, ident_raw[:])
         ident = keep.tile([P, P], F32, name="ident")
         nc.scalar.activation(ident[:], ident_raw[:], ACT.Relu)
 
@@ -141,11 +141,12 @@ def tile_moe_hot_mlp_relu2_kernel(
         def rectify(unit):
             for e in unit:
                 relu[e] = ring.tile([P, PACK, P], F32, name="relu")
-                src = pre[e][:].rearrange("s (m t) -> s t m", t=PACK)
+                src = pre[e][:].rearrange("s (b i t) -> s b t i", i=4, t=PACK)
+                dst = relu[e][:].rearrange("s t (b i) -> s b t i", i=4)
                 if e in RELU_ON_SCALAR:
-                    nc.scalar.activation(relu[e][:], src, ACT.Relu)
+                    nc.scalar.activation(dst, src, ACT.Relu)
                 else:
-                    nc.vector.tensor_scalar(relu[e][:], src, 0.0, None, ALU.max)
+                    nc.vector.tensor_scalar(dst, src, 0.0, None, ALU.max)
 
         def turn(unit):
             for e in unit:
@@ -160,8 +161,8 @@ def tile_moe_hot_mlp_relu2_kernel(
 
         def quantise(unit):
             width = len(unit) * C
-            h_words[unit] = ring.tile([P, 2 * C], U32, name="h_words", align_bytes=64)
-            h_scales[unit] = ring.tile([P, 2 * C], U8, name="h_scales", align_bytes=64)
+            h_words[unit] = codes.tile([P, 2 * C], U32, name="h_words", align_bytes=64)
+            h_scales[unit] = codes.tile([P, 2 * C], U8, name="h_scales", align_bytes=64)
             nc.vector.quantize_mx(
                 out=h_words[unit][:, :width].bitcast(FP8X4),
                 scales=h_scales[unit][:, :width],
@@ -187,23 +188,25 @@ def tile_moe_hot_mlp_relu2_kernel(
 
         def keep_results(unit):
             for half in range(N // P):
-                nc.scalar.copy(y[half][:, slots_of(unit)], y_bank[unit][:, half, : len(unit) * C])
+                src = y_bank[unit][:, half, : len(unit) * C]
+                if (unit[0], half) in KEEP_ON_VECTOR:
+                    nc.vector.tensor_copy(y[half][:, slots_of(unit)], src)
+                else:
+                    nc.scalar.copy(y[half][:, slots_of(unit)], src)
 
         def stage(work, index):
             if 0 <= index < len(UNITS):
                 work(UNITS[index])
 
-        gather_tokens(UNITS[0])
-        gather_tokens(UNITS[1])
-        for j in range(-1, len(UNITS) + 2):
-            stage(first_layer, j + 1)
-            stage(second_layer, j - 2)
+        for j in range(-4, len(UNITS) + 4):
             stage(square, j - 1)
-            stage(rectify, j + 1)
-            stage(keep_results, j - 2)
-            stage(gather_tokens, j + 3)
+            stage(second_layer, j - 3)
             stage(quantise, j - 1)
-            stage(turn, j)
+            stage(keep_results, j - 3)
+            stage(first_layer, j + 1)
+            stage(turn, j + 0)
+            stage(gather_tokens, j + 3)
+            stage(rectify, j + 1)
 
         positions = pos_sb
         terms = {}
@@ -214,19 +217,34 @@ def tile_moe_hot_mlp_relu2_kernel(
             entries = positions[r][:, t0 // LIST_ROWS : t1 // LIST_ROWS]
             nc.vector.tensor_tensor(terms[piece, r][:], y[half][:].indirect(entries), gate_sb[:, r, t0:t1], ALU.mult)
 
-        def add_first(piece):
-            nc.vector.tensor_tensor(terms[piece, 0][:], terms[piece, 0][:], terms[piece, 1][:], ALU.add)
-
-        def add_last(piece):
+        def add_on_tensor(piece, tags, back_pool, back_tag, back_shape):
             half, t0, t1 = piece
-            nc.vector.tensor_tensor(terms[piece, 0][:], terms[piece, 0][:], terms[piece, 2][:], ALU.add)
-            nc.sync.dma_start(out=out[half * P : (half + 1) * P, t0:t1], in_=terms[piece, 0][:])
+            blocks = (t1 - t0) // P
+            sums = [psum.tile([P, H], F32, name="sum_bank", tag=tags[b]) for b in range(blocks)]
+            for r in range(TOP):
+                fetch(piece, r)
+                for b in range(blocks):
+                    nc.tensor.matmul(
+                        sums[b][:, :P], lhsT=terms[piece, r][:, b * P : (b + 1) * P], rhs=ident[:],
+                        start=(r == 0), stop=(r == TOP - 1), is_transpose=True,
+                    )
+            by_token = keep.tile([P, blocks, P], F32, name="by_token_%d_%d" % (half, t0))
+            back = back_pool.tile([P, H], F32, name="back_bank", tag=back_tag)
+            for b in range(blocks):
+                nc.scalar.copy(by_token[:, b, :], sums[b][:, :P])
+                nc.tensor.transpose(back[:, b * P : (b + 1) * P], by_token[:, b, :], ident[:])
+            result = keep.tile([P, t1 - t0], F32, name="result_%d_%d" % (half, t0))
+            nc.scalar.copy(result[:], back[:, : t1 - t0])
+            nc.sync.dma_start(out=out[half * P : (half + 1) * P, t0:t1], in_=result[:])
 
-        for index, piece in enumerate(TAIL):
-            fetch(piece, 0)
-            if index > 0:
-                add_last(TAIL[index - 1])
-            fetch(piece, 1)
-            fetch(piece, 2)
-            add_first(piece)
-        add_last(TAIL[-1])
+        add_on_tensor((0, 0, 384), ("pre", "pre", "pre"), psum_y, "y_bank", None)
+        add_on_tensor((0, 384, 640), ("turned", "turned"), psum_y, "y_bank", None)
+        add_on_tensor((1, 0, 256), ("turned", "pre"), psum_y, "y_bank", None)
+        last = (1, 256, 640)
+        for r in range(TOP):
+            fetch(last, r)
+        parts = (slice(0, 192), slice(192, 384))
+        for r in (1, 2):
+            for part in parts:
+                nc.vector.tensor_tensor(terms[last, 0][:, part], terms[last, 0][:, part], terms[last, r][:, part], ALU.add)
+        nc.sync.dma_start(out=out[P:, 256:], in_=terms[last, 0][:])

@@ -22,11 +22,19 @@ ALU = mybir.AluOpType
 P = 128
 PACK = 4
 LIST_ROWS = 16
+QUADRANT = 32
+SCALE_ROWS = 4
+BANK = 512
+HALVES = N // P
 
-UNITS = [(7, 8), (9, 10), (11, 12), (13, 14), (0, 1), (2, 3), (4, 5), (6,)]
+UNIT = 2
+UNITS = [tuple(range(e, min(e + UNIT, end))) for first, end in ((HOT, E), (0, HOT)) for e in range(first, end, UNIT)]
+
 RELU_ON_SCALAR = (0, 1, 2, 7, 8, 9, 13, 14)
 KEEP_ON_VECTOR = ((7, 0), (7, 1), (9, 0), (9, 1), (11, 1), (13, 1), (0, 1), (4, 1))
-TAIL = [(0, 0, 640), (1, 0, 384), (1, 384, 640)]
+
+TENSOR_PIECES = ((0, 0, 384), (0, 384, 640), (1, 0, 256))
+LAST_PIECE = (1, 256, 640)
 
 
 def tile_moe_hot_mlp_relu2_kernel(
@@ -36,104 +44,108 @@ def tile_moe_hot_mlp_relu2_kernel(
     nc = tc.nc
     with ExitStack() as ctx:
         keep = ctx.enter_context(tc.tile_pool(name="keep", bufs=1))
+        word_ring = ctx.enter_context(tc.tile_pool(name="word_ring", bufs=3))
+        byte_ring = ctx.enter_context(tc.tile_pool(name="byte_ring", bufs=3))
         ring = ctx.enter_context(tc.tile_pool(name="ring", bufs=4))
-        slot_ring = ctx.enter_context(tc.tile_pool(name="slot_ring", bufs=3))
         codes = ctx.enter_context(tc.tile_pool(name="codes", bufs=len(UNITS)))
         psum = ctx.enter_context(tc.psum_pool(name="psum", bufs=3))
         psum_y = ctx.enter_context(tc.psum_pool(name="psum_y", bufs=2))
 
         offs_sb = keep.tile([P, SLOTS // LIST_ROWS], U16, name="offs_sb")
         pos_sb = [keep.tile([P, T // LIST_ROWS], U16, name="pos_sb%d" % r) for r in range(TOP)]
-        x_win = keep.tile([P, T], I32, name="x_win", align_bytes=64)
-        xs_win = keep.tile([P, 1, T], U8, name="xs_win", align_bytes=64)
-        s1h = keep.tile([P, HOT, H], U8, name="s1h", align_bytes=64)
-        s2h = keep.tile([P, HOT, N], U8, name="s2h", align_bytes=64)
-        s1c = keep.tile([P, E - HOT, H], U8, name="s1c", align_bytes=64)
-        s2c = keep.tile([P, E - HOT, N], U8, name="s2c", align_bytes=64)
+        x_window = keep.tile([P, T], I32, name="x_window", align_bytes=64)
         gate_sb = keep.tile([P, TOP, T], F32, name="gate_sb")
-        y = [keep.tile([P, SLOTS], F32, name="y%d" % half) for half in range(N // P)]
+        y = [keep.tile([P, SLOTS], F32, name="y%d" % half) for half in range(HALVES)]
 
-        for plane in (xs_win, s1c, s2c, s1h, s2h):
-            nc.vector.memset(plane[:].bitcast(I32), 0)
+        def zeroed_planes(label, count, width):
+            planes = keep.tile([P, count, width], U8, name=label, align_bytes=64)
+            nc.vector.memset(planes[:].bitcast(I32), 0)
+            return planes
 
-        def load_scales(plane, rows, queue=nc.sync, quadrants=(0, 2, 1, 3)):
+        def load_planes(queue, planes, rows, quadrants=(0, 2, 1, 3)):
             for q in quadrants:
-                queue.dma_start(out=plane[32 * q : 32 * q + 4, :, :].bitcast(I32), in_=rows[q].bitcast(I32))
+                live = planes[QUADRANT * q : QUADRANT * q + SCALE_ROWS, :, :]
+                queue.dma_start(out=live.bitcast(I32), in_=rows[q].bitcast(I32))
 
         def scale_rows(scales):
-            return scales.rearrange("e s (q r) n -> q r (e s) n", r=4)
+            return scales.rearrange("e s (q r) c -> q r (e s) c", r=SCALE_ROWS)
 
-        w1 = {}
-        w2 = {}
+        w1, w2 = {}, {}
 
-        def load_words(store, label, words_hot, words_cold, experts, queue):
-            first = experts[0]
+        def load_words(queue, store, label, hot, cold, first, end):
             if first < HOT:
-                src = words_hot.rearrange("e s p n d -> p (e s) (n d)")[:, first : first + len(experts), :]
+                src = hot.rearrange("e s p c d -> p (e s) (c d)")[:, first:end, :]
             else:
-                src = words_cold.rearrange("e s p n -> p (e s) n")[:, first - HOT : first - HOT + len(experts), :]
-            words = keep.tile([P, len(experts), src.shape[2]], U8, name="%s_%d" % (label, first), align_bytes=64)
+                src = cold.rearrange("e s p c -> p (e s) c")[:, first - HOT : end - HOT, :]
+            words = keep.tile([P, end - first, src.shape[2]], U8, name="%s_%d" % (label, first), align_bytes=64)
             queue.dma_start(out=words[:].bitcast(I32), in_=src.bitcast(I32))
-            for place, e in enumerate(experts):
-                store[e] = words[:, place, :]
+            for e in range(first, end):
+                store[e] = words[:, e - first, :]
 
-        ident_raw = keep.tile([P, P], F32, name="ident_raw")
-        x_rows = x_scales.rearrange("s (q r) t -> q r s t", r=4)
-        nc.scalar.dma_start(out=x_win[:], in_=x_words.rearrange("s p t d -> p (s t d)").bitcast(I32))
-        load_scales(xs_win, x_rows, nc.scalar, (1, 3))
-        load_words(w1, "w1", w1h_words, w1c_words, (7, 8, 9, 10), nc.gpsimd)
-        make_identity(nc, ident_raw[:])
-        load_words(w1, "w1", w1h_words, w1c_words, (11, 12, 13, 14), nc.gpsimd)
-        load_words(w2, "w2", w2h_words, w2c_words, tuple(range(HOT, E)), nc.gpsimd)
-        load_words(w1, "w1", w1h_words, w1c_words, (0, 1, 2, 3), nc.gpsimd)
-        load_words(w1, "w1", w1h_words, w1c_words, (4, 5, 6), nc.gpsimd)
-        load_words(w2, "w2", w2h_words, w2c_words, tuple(range(HOT)), nc.gpsimd)
+        x_plane = zeroed_planes("x_plane", 1, T)
+        s1_cold = zeroed_planes("s1_cold", E - HOT, H)
+        s1_hot = zeroed_planes("s1_hot", HOT, H)
+        s2_cold = zeroed_planes("s2_cold", E - HOT, N)
+        s2_hot = zeroed_planes("s2_hot", HOT, N)
+
+        identity_raw = keep.tile([P, P], F32, name="identity_raw")
+        make_identity(nc, identity_raw[:])
+
+        x_rows = x_scales.rearrange("s (q r) t -> q r s t", r=SCALE_ROWS)
+        nc.scalar.dma_start(out=x_window[:], in_=x_words.rearrange("s p t d -> p (s t d)").bitcast(I32))
+        load_planes(nc.scalar, x_plane, x_rows, (1, 3))
+        load_planes(nc.scalar, s1_cold, scale_rows(w1c_scales))
+        identity = keep.tile([P, P], F32, name="identity")
+        nc.scalar.activation(identity[:], identity_raw[:], ACT.Relu)
+        load_words(nc.scalar, w1, "w1", w1h_words, w1c_words, 0, 2)
+
         nc.sync.dma_start(offs_sb[:], offs)
-        load_scales(xs_win, x_rows, nc.sync, (0, 2))
-        load_scales(s1c, scale_rows(w1c_scales))
-        load_scales(s1h, scale_rows(w1h_scales))
-        load_scales(s2c, scale_rows(w2c_scales))
-        load_scales(s2h, scale_rows(w2h_scales))
-        for tile_r, pos in zip(pos_sb, (pos1, pos2, pos3)):
-            nc.sync.dma_start(tile_r[:], pos)
+        load_planes(nc.sync, x_plane, x_rows, (0, 2))
+        load_words(nc.sync, w1, "w1", w1h_words, w1c_words, HOT, HOT + 4)
+        load_planes(nc.sync, s1_hot, scale_rows(w1h_scales))
+        load_words(nc.sync, w1, "w1", w1h_words, w1c_words, HOT + 4, E)
+        load_planes(nc.sync, s2_cold, scale_rows(w2c_scales))
+        load_words(nc.sync, w2, "w2", w2h_words, w2c_words, HOT, E)
+        load_words(nc.sync, w1, "w1", w1h_words, w1c_words, 2, 4)
+        load_words(nc.sync, w1, "w1", w1h_words, w1c_words, 4, HOT)
+        load_planes(nc.sync, s2_hot, scale_rows(w2h_scales))
+        load_words(nc.sync, w2, "w2", w2h_words, w2c_words, 0, HOT)
+        for list_sb, pos in zip(pos_sb, (pos1, pos2, pos3)):
+            nc.sync.dma_start(list_sb[:], pos)
         nc.sync.dma_start(out=gate_sb[:], in_=gate.rearrange("r p t -> p r t"))
 
-        ident = keep.tile([P, P], F32, name="ident")
-        nc.scalar.activation(ident[:], ident_raw[:], ACT.Relu)
+        s1 = [s1_hot[:, e, :] for e in range(HOT)] + [s1_cold[:, e, :] for e in range(E - HOT)]
+        s2 = [s2_hot[:, e, :] for e in range(HOT)] + [s2_cold[:, e, :] for e in range(E - HOT)]
 
-        def fmt(e):
+        x_slot, x_slot_plane, v, relu, turned, h_bf, h_words, h_plane, y_bank = {}, {}, {}, {}, {}, {}, {}, {}, {}
+
+        def packed(e):
             return FP8X4 if e < HOT else FP4X4
 
-        def slots_of(experts):
-            return slice(experts[0] * C, (experts[-1] + 1) * C)
-
-        x_slot, xs_slot = {}, {}
+        def entries(list_sb, first, end):
+            return list_sb[:, first // LIST_ROWS : end // LIST_ROWS]
 
         def gather_tokens(unit):
-            words = slot_ring.tile([P, 2 * C], U32, name="slot_words", align_bytes=64)
-            scale_bytes = slot_ring.tile([P, 2 * C], U8, name="slot_bytes", align_bytes=64)
-            pieces = [(e,) for e in unit] if unit == UNITS[0] else [unit]
-            for piece in pieces:
-                cols = slots_of(piece)
-                entries = offs_sb[:, cols.start // LIST_ROWS : cols.stop // LIST_ROWS]
-                local = slice(cols.start - unit[0] * C, cols.stop - unit[0] * C)
-                nc.vector.tensor_copy(words[:, local], x_win[:].bitcast(U32).indirect(entries))
-                nc.vector.tensor_copy(scale_bytes[:, local], xs_win[:, 0, :].indirect(entries))
+            words = word_ring.tile([P, UNIT * C], U32, name="slot_words", align_bytes=64)
+            scale_bytes = byte_ring.tile([P, UNIT * C], U8, name="slot_bytes", align_bytes=64)
+            width = C if unit == UNITS[0] else len(unit) * C
+            for first in range(0, len(unit) * C, width):
+                listed = entries(offs_sb, unit[0] * C + first, unit[0] * C + first + width)
+                nc.vector.tensor_copy(words[:, first : first + width], x_window[:].bitcast(U32).indirect(listed))
+                nc.vector.tensor_copy(scale_bytes[:, first : first + width], x_plane[:, 0, :].indirect(listed))
             for place, e in enumerate(unit):
                 x_slot[e] = words[:, place * C : (place + 1) * C]
-                xs_slot[e] = scale_bytes[:, place * C : (place + 1) * C]
-
-        pre, relu, turned, h_bf, h_words, h_scales, y_bank = {}, {}, {}, {}, {}, {}, {}
+                x_slot_plane[e] = scale_bytes[:, place * C : (place + 1) * C]
 
         def first_layer(unit):
             for e in unit:
-                pre[e] = psum.tile([P, H], F32, name="pre")
+                v[e] = psum.tile([P, H], F32, name="v_bank", tag="v")
                 nc.tensor.matmul_mx(
-                    out=pre[e][:],
+                    out=v[e][:],
                     lhsT=x_slot[e].bitcast(FP8X4),
-                    lhsT_scale=xs_slot[e],
-                    rhs=w1[e].bitcast(fmt(e)),
-                    rhs_scale=s1h[:, e, :] if e < HOT else s1c[:, e - HOT, :],
+                    lhsT_scale=x_slot_plane[e],
+                    rhs=w1[e].bitcast(packed(e)),
+                    rhs_scale=s1[e],
                     start=True,
                     stop=True,
                 )
@@ -141,8 +153,8 @@ def tile_moe_hot_mlp_relu2_kernel(
         def rectify(unit):
             for e in unit:
                 relu[e] = ring.tile([P, PACK, P], F32, name="relu")
-                src = pre[e][:].rearrange("s (b i t) -> s b t i", i=4, t=PACK)
-                dst = relu[e][:].rearrange("s t (b i) -> s b t i", i=4)
+                src = v[e][:].rearrange("s (b a t) -> s b t a", a=4, t=PACK)
+                dst = relu[e][:].rearrange("s t (b a) -> s b t a", a=4)
                 if e in RELU_ON_SCALAR:
                     nc.scalar.activation(dst, src, ACT.Relu)
                 else:
@@ -150,101 +162,106 @@ def tile_moe_hot_mlp_relu2_kernel(
 
         def turn(unit):
             for e in unit:
-                turned[e] = psum.tile([P, PACK, C], F32, name="turned")
+                turned[e] = psum.tile([P, PACK, C], F32, name="turned_bank", tag="turned")
                 for t in range(PACK):
-                    nc.tensor.transpose(turned[e][:, t, :], relu[e][:, t, :], ident[:])
+                    nc.tensor.transpose(turned[e][:, t, :], relu[e][:, t, :], identity[:])
 
         def square(unit):
-            h_bf[unit] = ring.tile([P, 2, C, PACK], BF16, name="h_bf", align_bytes=64)
+            h_bf[unit] = ring.tile([P, UNIT, C, PACK], BF16, name="h_bf", align_bytes=64)
             for place, e in enumerate(unit):
                 nc.scalar.activation(h_bf[unit][:, place, :, :], turned[e][:].rearrange("m t s -> m s t"), ACT.Square)
 
         def quantise(unit):
             width = len(unit) * C
-            h_words[unit] = codes.tile([P, 2 * C], U32, name="h_words", align_bytes=64)
-            h_scales[unit] = codes.tile([P, 2 * C], U8, name="h_scales", align_bytes=64)
+            h_words[unit] = codes.tile([P, UNIT * C], U32, name="h_words", align_bytes=64)
+            h_plane[unit] = codes.tile([P, UNIT * C], U8, name="h_plane", align_bytes=64)
             nc.vector.quantize_mx(
                 out=h_words[unit][:, :width].bitcast(FP8X4),
-                scales=h_scales[unit][:, :width],
+                scales=h_plane[unit][:, :width],
                 in_=h_bf[unit][:].rearrange("m e s t -> m (e s t)")[:, : width * PACK],
             )
 
         def second_layer(unit):
-            y_bank[unit] = psum_y.tile([P, N // P, 2 * C], F32, name="y_bank")
-            for half in range(N // P):
+            y_bank[unit] = psum_y.tile([P, HALVES, UNIT * C], F32, name="y_bank", tag="y")
+            for half in range(HALVES):
+                rows = slice(half * P, (half + 1) * P)
                 for place, e in enumerate(unit):
-                    word_bytes = 4 if e < HOT else 2
+                    word_bytes = w2[e].shape[1] // N
                     cols = slice(place * C, (place + 1) * C)
-                    plane = s2h[:, e, :] if e < HOT else s2c[:, e - HOT, :]
                     nc.tensor.matmul_mx(
                         out=y_bank[unit][:, half, cols],
-                        lhsT=w2[e][:, half * P * word_bytes : (half + 1) * P * word_bytes].bitcast(fmt(e)),
-                        lhsT_scale=plane[:, half * P : (half + 1) * P],
+                        lhsT=w2[e][:, rows.start * word_bytes : rows.stop * word_bytes].bitcast(packed(e)),
+                        lhsT_scale=s2[e][:, rows],
                         rhs=h_words[unit][:, cols].bitcast(FP8X4),
-                        rhs_scale=h_scales[unit][:, cols],
+                        rhs_scale=h_plane[unit][:, cols],
                         start=True,
                         stop=True,
                     )
 
         def keep_results(unit):
-            for half in range(N // P):
+            for half in range(HALVES):
+                dst = y[half][:, unit[0] * C : (unit[-1] + 1) * C]
                 src = y_bank[unit][:, half, : len(unit) * C]
                 if (unit[0], half) in KEEP_ON_VECTOR:
-                    nc.vector.tensor_copy(y[half][:, slots_of(unit)], src)
+                    nc.vector.tensor_copy(dst, src)
                 else:
-                    nc.scalar.copy(y[half][:, slots_of(unit)], src)
+                    nc.scalar.copy(dst, src)
 
-        def stage(work, index):
-            if 0 <= index < len(UNITS):
-                work(UNITS[index])
+        leads = (
+            (square, -1),
+            (second_layer, -3),
+            (quantise, -1),
+            (keep_results, -3),
+            (first_layer, 1),
+            (turn, 0),
+            (gather_tokens, 3),
+            (rectify, 1),
+        )
+        for j in range(-max(lead for stage, lead in leads), len(UNITS) - min(lead for stage, lead in leads)):
+            for stage, lead in leads:
+                if 0 <= j + lead < len(UNITS):
+                    stage(UNITS[j + lead])
 
-        for j in range(-4, len(UNITS) + 4):
-            stage(square, j - 1)
-            stage(second_layer, j - 3)
-            stage(quantise, j - 1)
-            stage(keep_results, j - 3)
-            stage(first_layer, j + 1)
-            stage(turn, j + 0)
-            stage(gather_tokens, j + 3)
-            stage(rectify, j + 1)
+        def fetch_term(piece, r):
+            half, first, end = piece
+            term = keep.tile([P, end - first], F32, name="term_%d_%d_%d" % (half, first, r))
+            listed = entries(pos_sb[r], first, end)
+            nc.vector.tensor_tensor(term[:], y[half][:].indirect(listed), gate_sb[:, r, first:end], ALU.mult)
+            return term
 
-        positions = pos_sb
-        terms = {}
-
-        def fetch(piece, r):
-            half, t0, t1 = piece
-            terms[piece, r] = keep.tile([P, t1 - t0], F32, name="term_%d_%d_%d" % (half, t0, r))
-            entries = positions[r][:, t0 // LIST_ROWS : t1 // LIST_ROWS]
-            nc.vector.tensor_tensor(terms[piece, r][:], y[half][:].indirect(entries), gate_sb[:, r, t0:t1], ALU.mult)
-
-        def add_on_tensor(piece, tags, back_pool, back_tag, back_shape):
-            half, t0, t1 = piece
-            blocks = (t1 - t0) // P
-            sums = [psum.tile([P, H], F32, name="sum_bank", tag=tags[b]) for b in range(blocks)]
+        block_count = 0
+        for piece in TENSOR_PIECES:
+            half, first, end = piece
+            blocks = (end - first) // P
+            sums = []
+            for b in range(blocks):
+                tag = ("v", "turned")[block_count // 3 % 2]
+                block_count += 1
+                sums.append(psum.tile([P, BANK], F32, name="sum_bank", tag=tag))
             for r in range(TOP):
-                fetch(piece, r)
+                term = fetch_term(piece, r)
                 for b in range(blocks):
                     nc.tensor.matmul(
-                        sums[b][:, :P], lhsT=terms[piece, r][:, b * P : (b + 1) * P], rhs=ident[:],
-                        start=(r == 0), stop=(r == TOP - 1), is_transpose=True,
+                        sums[b][:, :P],
+                        lhsT=term[:, b * P : (b + 1) * P],
+                        rhs=identity[:],
+                        start=(r == 0),
+                        stop=(r == TOP - 1),
+                        is_transpose=True,
                     )
-            by_token = keep.tile([P, blocks, P], F32, name="by_token_%d_%d" % (half, t0))
-            back = back_pool.tile([P, H], F32, name="back_bank", tag=back_tag)
+            by_token = keep.tile([P, blocks, P], F32, name="by_token_%d_%d" % (half, first))
+            back = psum_y.tile([P, BANK], F32, name="back_bank", tag="y")
             for b in range(blocks):
                 nc.scalar.copy(by_token[:, b, :], sums[b][:, :P])
-                nc.tensor.transpose(back[:, b * P : (b + 1) * P], by_token[:, b, :], ident[:])
-            result = keep.tile([P, t1 - t0], F32, name="result_%d_%d" % (half, t0))
-            nc.scalar.copy(result[:], back[:, : t1 - t0])
-            nc.sync.dma_start(out=out[half * P : (half + 1) * P, t0:t1], in_=result[:])
+                nc.tensor.transpose(back[:, b * P : (b + 1) * P], by_token[:, b, :], identity[:])
+            result = keep.tile([P, end - first], F32, name="result_%d_%d" % (half, first))
+            nc.scalar.copy(result[:], back[:, : end - first])
+            nc.sync.dma_start(out=out[half * P : (half + 1) * P, first:end], in_=result[:])
 
-        add_on_tensor((0, 0, 384), ("pre", "pre", "pre"), psum_y, "y_bank", None)
-        add_on_tensor((0, 384, 640), ("turned", "turned"), psum_y, "y_bank", None)
-        add_on_tensor((1, 0, 256), ("turned", "pre"), psum_y, "y_bank", None)
-        last = (1, 256, 640)
-        for r in range(TOP):
-            fetch(last, r)
-        parts = (slice(0, 192), slice(192, 384))
-        for r in (1, 2):
-            for part in parts:
-                nc.vector.tensor_tensor(terms[last, 0][:, part], terms[last, 0][:, part], terms[last, r][:, part], ALU.add)
-        nc.sync.dma_start(out=out[P:, 256:], in_=terms[last, 0][:])
+        half, first, end = LAST_PIECE
+        terms = [fetch_term(LAST_PIECE, r) for r in range(TOP)]
+        middle = (end - first) // 2
+        for r in range(1, TOP):
+            for part in (slice(0, middle), slice(middle, end - first)):
+                nc.vector.tensor_tensor(terms[0][:, part], terms[0][:, part], terms[r][:, part], ALU.add)
+        nc.sync.dma_start(out=out[half * P : (half + 1) * P, first:end], in_=terms[0][:])

@@ -30,8 +30,8 @@ HALVES = N // P
 UNIT = 2
 UNITS = [tuple(range(e, min(e + UNIT, end))) for first, end in ((HOT, E), (0, HOT)) for e in range(first, end, UNIT)]
 
-RELU_ON_SCALAR = (0, 1, 2, 7, 8, 9, 13, 14)
-KEEP_ON_VECTOR = ((7, 0), (7, 1), (9, 0), (9, 1), (11, 1), (13, 1), (0, 1), (4, 1))
+RELU_ON_SCALAR = (8, 9, 10, 12, 13, 14, 0, 5)
+KEEP_ON_VECTOR = (7, 9, 11, 13, 0, 6)
 
 TENSOR_PIECES = ((0, 0, 384), (0, 384, 640), (1, 0, 256))
 LAST_PIECE = (1, 256, 640)
@@ -44,11 +44,12 @@ def tile_moe_hot_mlp_relu2_kernel(
     nc = tc.nc
     with ExitStack() as ctx:
         keep = ctx.enter_context(tc.tile_pool(name="keep", bufs=1))
-        word_ring = ctx.enter_context(tc.tile_pool(name="word_ring", bufs=3))
-        byte_ring = ctx.enter_context(tc.tile_pool(name="byte_ring", bufs=3))
-        ring = ctx.enter_context(tc.tile_pool(name="ring", bufs=4))
+        word_ring = ctx.enter_context(tc.tile_pool(name="word_ring", bufs=2))
+        byte_ring = ctx.enter_context(tc.tile_pool(name="byte_ring", bufs=4))
+        relu_ring = ctx.enter_context(tc.tile_pool(name="relu_ring", bufs=4))
+        h_ring = ctx.enter_context(tc.tile_pool(name="h_ring", bufs=3))
         codes = ctx.enter_context(tc.tile_pool(name="codes", bufs=len(UNITS)))
-        psum = ctx.enter_context(tc.psum_pool(name="psum", bufs=3))
+        psum_v = ctx.enter_context(tc.psum_pool(name="psum_v", bufs=3))
         psum_y = ctx.enter_context(tc.psum_pool(name="psum_y", bufs=2))
 
         offs_sb = keep.tile([P, SLOTS // LIST_ROWS], U16, name="offs_sb")
@@ -72,15 +73,27 @@ def tile_moe_hot_mlp_relu2_kernel(
 
         w1, w2 = {}, {}
 
-        def load_words(queue, store, label, hot, cold, first, end):
+        def expert_words(hot, cold, first, end):
             if first < HOT:
-                src = hot.rearrange("e s p c d -> p (e s) (c d)")[:, first:end, :]
-            else:
-                src = cold.rearrange("e s p c -> p (e s) c")[:, first - HOT : end - HOT, :]
-            words = keep.tile([P, end - first, src.shape[2]], U8, name="%s_%d" % (label, first), align_bytes=64)
+                return hot.rearrange("e s p c d -> p (e s) (c d)")[:, first:end, :]
+            return cold.rearrange("e s p c -> p (e s) c")[:, first - HOT : end - HOT, :]
+
+        def load_words(queue, label, src):
+            words = keep.tile(list(src.shape), U8, name=label, align_bytes=64)
             queue.dma_start(out=words[:].bitcast(I32), in_=src.bitcast(I32))
+            return words
+
+        def load_w1(queue, first, end):
+            words = load_words(queue, "w1_%d" % first, expert_words(w1h_words, w1c_words, first, end))
             for e in range(first, end):
-                store[e] = words[:, e - first, :]
+                w1[e] = words[:, e - first, :]
+
+        def load_w2(queue, first, end, half):
+            src = expert_words(w2h_words, w2c_words, first, end)
+            half_bytes = src.shape[2] // HALVES
+            words = load_words(queue, "w2_%d_%d" % (first, half), src[:, :, half * half_bytes : (half + 1) * half_bytes])
+            for e in range(first, end):
+                w2[e, half] = words[:, e - first, :]
 
         x_plane = zeroed_planes("x_plane", 1, T)
         s1_cold = zeroed_planes("s1_cold", E - HOT, H)
@@ -97,19 +110,21 @@ def tile_moe_hot_mlp_relu2_kernel(
         load_planes(nc.scalar, s1_cold, scale_rows(w1c_scales))
         identity = keep.tile([P, P], F32, name="identity")
         nc.scalar.activation(identity[:], identity_raw[:], ACT.Relu)
-        load_words(nc.scalar, w1, "w1", w1h_words, w1c_words, 0, 2)
+        load_w1(nc.scalar, 0, 2)
 
         nc.sync.dma_start(offs_sb[:], offs)
         load_planes(nc.sync, x_plane, x_rows, (0, 2))
-        load_words(nc.sync, w1, "w1", w1h_words, w1c_words, HOT, HOT + 4)
+        load_w1(nc.sync, HOT, HOT + 4)
         load_planes(nc.sync, s1_hot, scale_rows(w1h_scales))
-        load_words(nc.sync, w1, "w1", w1h_words, w1c_words, HOT + 4, E)
+        load_w1(nc.sync, HOT + 4, E)
+        load_w1(nc.sync, 2, 4)
         load_planes(nc.sync, s2_cold, scale_rows(w2c_scales))
-        load_words(nc.sync, w2, "w2", w2h_words, w2c_words, HOT, E)
-        load_words(nc.sync, w1, "w1", w1h_words, w1c_words, 2, 4)
-        load_words(nc.sync, w1, "w1", w1h_words, w1c_words, 4, HOT)
+        load_w2(nc.sync, HOT, E, 0)
+        load_w1(nc.sync, 4, HOT)
         load_planes(nc.sync, s2_hot, scale_rows(w2h_scales))
-        load_words(nc.sync, w2, "w2", w2h_words, w2c_words, 0, HOT)
+        load_w2(nc.sync, 0, HOT, 0)
+        load_w2(nc.sync, HOT, E, 1)
+        load_w2(nc.sync, 0, HOT, 1)
         for list_sb, pos in zip(pos_sb, (pos1, pos2, pos3)):
             nc.sync.dma_start(list_sb[:], pos)
         nc.sync.dma_start(out=gate_sb[:], in_=gate.rearrange("r p t -> p r t"))
@@ -139,7 +154,7 @@ def tile_moe_hot_mlp_relu2_kernel(
 
         def first_layer(unit):
             for e in unit:
-                v[e] = psum.tile([P, H], F32, name="v_bank", tag="v")
+                v[e] = psum_v.tile([P, H], F32, name="v_bank", tag="v")
                 nc.tensor.matmul_mx(
                     out=v[e][:],
                     lhsT=x_slot[e].bitcast(FP8X4),
@@ -152,7 +167,7 @@ def tile_moe_hot_mlp_relu2_kernel(
 
         def rectify(unit):
             for e in unit:
-                relu[e] = ring.tile([P, PACK, P], F32, name="relu")
+                relu[e] = relu_ring.tile([P, PACK, P], F32, name="relu")
                 src = v[e][:].rearrange("s (b a t) -> s b t a", a=4, t=PACK)
                 dst = relu[e][:].rearrange("s t (b a) -> s b t a", a=4)
                 if e in RELU_ON_SCALAR:
@@ -162,12 +177,12 @@ def tile_moe_hot_mlp_relu2_kernel(
 
         def turn(unit):
             for e in unit:
-                turned[e] = psum.tile([P, PACK, C], F32, name="turned_bank", tag="turned")
+                turned[e] = psum_turned.tile([P, PACK, C], F32, name="turned_bank")
                 for t in range(PACK):
                     nc.tensor.transpose(turned[e][:, t, :], relu[e][:, t, :], identity[:])
 
         def square(unit):
-            h_bf[unit] = ring.tile([P, UNIT, C, PACK], BF16, name="h_bf", align_bytes=64)
+            h_bf[unit] = h_ring.tile([P, UNIT, C, PACK], BF16, name="h_bf", align_bytes=64)
             for place, e in enumerate(unit):
                 nc.scalar.activation(h_bf[unit][:, place, :, :], turned[e][:].rearrange("m t s -> m s t"), ACT.Square)
 
@@ -181,46 +196,54 @@ def tile_moe_hot_mlp_relu2_kernel(
                 in_=h_bf[unit][:].rearrange("m e s t -> m (e s t)")[:, : width * PACK],
             )
 
+        def second_product(unit, half, bank):
+            rows = slice(half * P, (half + 1) * P)
+            for place, e in enumerate(unit):
+                cols = slice(place * C, (place + 1) * C)
+                nc.tensor.matmul_mx(
+                    out=bank[:, cols],
+                    lhsT=w2[e, half].bitcast(packed(e)),
+                    lhsT_scale=s2[e][:, rows],
+                    rhs=h_words[unit][:, cols].bitcast(FP8X4),
+                    rhs_scale=h_plane[unit][:, cols],
+                    start=True,
+                    stop=True,
+                )
+
         def second_layer(unit):
-            y_bank[unit] = psum_y.tile([P, HALVES, UNIT * C], F32, name="y_bank", tag="y")
-            for half in range(HALVES):
-                rows = slice(half * P, (half + 1) * P)
-                for place, e in enumerate(unit):
-                    word_bytes = w2[e].shape[1] // N
-                    cols = slice(place * C, (place + 1) * C)
-                    nc.tensor.matmul_mx(
-                        out=y_bank[unit][:, half, cols],
-                        lhsT=w2[e][:, rows.start * word_bytes : rows.stop * word_bytes].bitcast(packed(e)),
-                        lhsT_scale=s2[e][:, rows],
-                        rhs=h_words[unit][:, cols].bitcast(FP8X4),
-                        rhs_scale=h_plane[unit][:, cols],
-                        start=True,
-                        stop=True,
-                    )
+            y_bank[unit] = psum_y.tile([P, UNIT * C], F32, name="y_bank", tag="y")
+            second_product(unit, 0, y_bank[unit][:])
 
         def keep_results(unit):
-            for half in range(HALVES):
-                dst = y[half][:, unit[0] * C : (unit[-1] + 1) * C]
-                src = y_bank[unit][:, half, : len(unit) * C]
-                if (unit[0], half) in KEEP_ON_VECTOR:
-                    nc.vector.tensor_copy(dst, src)
-                else:
-                    nc.scalar.copy(dst, src)
+            dst = y[0][:, unit[0] * C : (unit[-1] + 1) * C]
+            src = y_bank[unit][:, : len(unit) * C]
+            if unit[0] in KEEP_ON_VECTOR:
+                nc.vector.tensor_copy(dst, src)
+            else:
+                nc.scalar.copy(dst, src)
 
         leads = (
-            (square, -1),
             (second_layer, -3),
-            (quantise, -1),
-            (keep_results, -3),
+            (gather_tokens, 1),
+            (quantise, -2),
+            (rectify, 0),
+            (square, -1),
+            (keep_results, -4),
             (first_layer, 1),
             (turn, 0),
-            (gather_tokens, 3),
-            (rectify, 1),
         )
-        for j in range(-max(lead for stage, lead in leads), len(UNITS) - min(lead for stage, lead in leads)):
-            for stage, lead in leads:
-                if 0 <= j + lead < len(UNITS):
-                    stage(UNITS[j + lead])
+        with tc.psum_pool(name="psum_turned", bufs=3) as psum_turned:
+            for j in range(-max(lead for stage, lead in leads), len(UNITS) - min(lead for stage, lead in leads)):
+                for stage, lead in leads:
+                    if 0 <= j + lead < len(UNITS):
+                        stage(UNITS[j + lead])
+
+        psum_late = ctx.enter_context(tc.psum_pool(name="psum_late", bufs=3))
+        for one, other in zip(UNITS[0::2], UNITS[1::2]):
+            bank = psum_late.tile([P, BANK], F32, name="late_bank", tag="late")
+            second_product(one, 1, bank[:, : UNIT * C])
+            second_product(other, 1, bank[:, UNIT * C :])
+            nc.scalar.copy(y[1][:, one[0] * C : (other[-1] + 1) * C], bank[:, : (len(one) + len(other)) * C])
 
         def fetch_term(piece, r):
             half, first, end = piece
@@ -229,15 +252,11 @@ def tile_moe_hot_mlp_relu2_kernel(
             nc.vector.tensor_tensor(term[:], y[half][:].indirect(listed), gate_sb[:, r, first:end], ALU.mult)
             return term
 
-        block_count = 0
-        for piece in TENSOR_PIECES:
+        for index, piece in enumerate(TENSOR_PIECES):
             half, first, end = piece
             blocks = (end - first) // P
-            sums = []
-            for b in range(blocks):
-                tag = ("v", "turned")[block_count // 3 % 2]
-                block_count += 1
-                sums.append(psum.tile([P, BANK], F32, name="sum_bank", tag=tag))
+            pool, tag = ((psum_v, "v"), (psum_late, "late"))[index % 2]
+            sums = [pool.tile([P, BANK], F32, name="sum_bank", tag=tag) for b in range(blocks)]
             for r in range(TOP):
                 term = fetch_term(piece, r)
                 for b in range(blocks):

from contextlib import ExitStack

import concourse.mybir as mybir
from concourse.masks import make_identity

K, T, E, C, H, N, HOT = 512, 640, 15, 128, 512, 256, 7
TOP = 3
SLOTS = E * C
FLOPS = 2 * SLOTS * (K * H + H * N)

F32 = mybir.dt.float32
BF16 = mybir.dt.bfloat16
I32 = mybir.dt.int32
U32 = mybir.dt.uint32
U16 = mybir.dt.uint16
U8 = mybir.dt.uint8
FP8X4 = mybir.dt.float8_e4m3fn_x4
FP4X4 = mybir.dt.float4_e2m1fn_x4
ACT = mybir.ActivationFunctionType
ALU = mybir.AluOpType

P = 128
PACK = 4
LIST_ROWS = 16
QUADRANT = 32
SCALE_ROWS = 4
BANK = 512
HALVES = N // P

UNIT = 2
UNITS = [tuple(range(e, min(e + UNIT, end))) for first, end in ((HOT, E), (0, HOT)) for e in range(first, end, UNIT)]

RELU_ON_SCALAR = (8, 9, 10, 12, 13, 14, 0, 5)
KEEP_ON_VECTOR = (7, 9, 11, 13, 0, 6)

TENSOR_PIECES = ((0, 0, 384), (0, 384, 640), (1, 0, 256))
LAST_PIECE = (1, 256, 640)


def tile_moe_hot_mlp_relu2_kernel(
    tc, x_words, x_scales, w1h_words, w1h_scales, w2h_words, w2h_scales,
    w1c_words, w1c_scales, w2c_words, w2c_scales, gate, offs, pos1, pos2, pos3, out,
):
    nc = tc.nc
    with ExitStack() as ctx:
        keep = ctx.enter_context(tc.tile_pool(name="keep", bufs=1))
        word_ring = ctx.enter_context(tc.tile_pool(name="word_ring", bufs=2))
        byte_ring = ctx.enter_context(tc.tile_pool(name="byte_ring", bufs=4))
        relu_ring = ctx.enter_context(tc.tile_pool(name="relu_ring", bufs=4))
        h_ring = ctx.enter_context(tc.tile_pool(name="h_ring", bufs=3))
        codes = ctx.enter_context(tc.tile_pool(name="codes", bufs=len(UNITS)))
        psum_v = ctx.enter_context(tc.psum_pool(name="psum_v", bufs=3))
        psum_y = ctx.enter_context(tc.psum_pool(name="psum_y", bufs=2))

        offs_sb = keep.tile([P, SLOTS // LIST_ROWS], U16, name="offs_sb")
        pos_sb = [keep.tile([P, T // LIST_ROWS], U16, name="pos_sb%d" % r) for r in range(TOP)]
        x_window = keep.tile([P, T], I32, name="x_window", align_bytes=64)
        gate_sb = keep.tile([P, TOP, T], F32, name="gate_sb")
        y = [keep.tile([P, SLOTS], F32, name="y%d" % half) for half in range(HALVES)]

        def zeroed_planes(label, count, width):
            planes = keep.tile([P, count, width], U8, name=label, align_bytes=64)
            nc.vector.memset(planes[:].bitcast(I32), 0)
            return planes

        def load_planes(queue, planes, rows, quadrants=(0, 2, 1, 3)):
            for q in quadrants:
                live = planes[QUADRANT * q : QUADRANT * q + SCALE_ROWS, :, :]
                queue.dma_start(out=live.bitcast(I32), in_=rows[q].bitcast(I32))

        def scale_rows(scales):
            return scales.rearrange("e s (q r) c -> q r (e s) c", r=SCALE_ROWS)

        w1, w2 = {}, {}

        def expert_words(hot, cold, first, end):
            if first < HOT:
                return hot.rearrange("e s p c d -> p (e s) (c d)")[:, first:end, :]
            return cold.rearrange("e s p c -> p (e s) c")[:, first - HOT : end - HOT, :]

        def load_words(queue, label, src):
            words = keep.tile(list(src.shape), U8, name=label, align_bytes=64)
            queue.dma_start(out=words[:].bitcast(I32), in_=src.bitcast(I32))
            return words

        def load_w1(queue, first, end):
            words = load_words(queue, "w1_%d" % first, expert_words(w1h_words, w1c_words, first, end))
            for e in range(first, end):
                w1[e] = words[:, e - first, :]

        def load_w2(queue, first, end, half):
            src = expert_words(w2h_words, w2c_words, first, end)
            half_bytes = src.shape[2] // HALVES
            words = load_words(queue, "w2_%d_%d" % (first, half), src[:, :, half * half_bytes : (half + 1) * half_bytes])
            for e in range(first, end):
                w2[e, half] = words[:, e - first, :]

        x_plane = zeroed_planes("x_plane", 1, T)
        s1_cold = zeroed_planes("s1_cold", E - HOT, H)
        s1_hot = zeroed_planes("s1_hot", HOT, H)
        s2_cold = zeroed_planes("s2_cold", E - HOT, N)
        s2_hot = zeroed_planes("s2_hot", HOT, N)

        identity_raw = keep.tile([P, P], F32, name="identity_raw")
        make_identity(nc, identity_raw[:])

        x_rows = x_scales.rearrange("s (q r) t -> q r s t", r=SCALE_ROWS)
        nc.scalar.dma_start(out=x_window[:], in_=x_words.rearrange("s p t d -> p (s t d)").bitcast(I32))
        load_planes(nc.scalar, x_plane, x_rows, (1, 3))
        load_planes(nc.scalar, s1_cold, scale_rows(w1c_scales))
        identity = keep.tile([P, P], F32, name="identity")
        nc.scalar.activation(identity[:], identity_raw[:], ACT.Relu)
        load_w1(nc.scalar, 0, 2)

        nc.sync.dma_start(offs_sb[:], offs)
        load_planes(nc.sync, x_plane, x_rows, (0, 2))
        load_w1(nc.sync, HOT, HOT + 4)
        load_planes(nc.sync, s1_hot, scale_rows(w1h_scales))
        load_w1(nc.sync, HOT + 4, E)
        load_w1(nc.sync, 2, 4)
        load_planes(nc.sync, s2_cold, scale_rows(w2c_scales))
        load_w2(nc.sync, HOT, E, 0)
        load_w1(nc.sync, 4, HOT)
        load_planes(nc.sync, s2_hot, scale_rows(w2h_scales))
        load_w2(nc.sync, 0, HOT, 0)
        load_w2(nc.sync, HOT, E, 1)
        load_w2(nc.sync, 0, HOT, 1)
        for list_sb, pos in zip(pos_sb, (pos1, pos2, pos3)):
            nc.sync.dma_start(list_sb[:], pos)
        nc.sync.dma_start(out=gate_sb[:], in_=gate.rearrange("r p t -> p r t"))

        s1 = [s1_hot[:, e, :] for e in range(HOT)] + [s1_cold[:, e, :] for e in range(E - HOT)]
        s2 = [s2_hot[:, e, :] for e in range(HOT)] + [s2_cold[:, e, :] for e in range(E - HOT)]

        x_slot, x_slot_plane, v, relu, turned, h_bf, h_words, h_plane, y_bank = {}, {}, {}, {}, {}, {}, {}, {}, {}

        def packed(e):
            return FP8X4 if e < HOT else FP4X4

        def entries(list_sb, first, end):
            return list_sb[:, first // LIST_ROWS : end // LIST_ROWS]

        def gather_tokens(unit):
            words = word_ring.tile([P, UNIT * C], U32, name="slot_words", align_bytes=64)
            scale_bytes = byte_ring.tile([P, UNIT * C], U8, name="slot_bytes", align_bytes=64)
            width = C if unit == UNITS[0] else len(unit) * C
            for first in range(0, len(unit) * C, width):
                listed = entries(offs_sb, unit[0] * C + first, unit[0] * C + first + width)
                nc.vector.tensor_copy(words[:, first : first + width], x_window[:].bitcast(U32).indirect(listed))
                nc.vector.tensor_copy(scale_bytes[:, first : first + width], x_plane[:, 0, :].indirect(listed))
            for place, e in enumerate(unit):
                x_slot[e] = words[:, place * C : (place + 1) * C]
                x_slot_plane[e] = scale_bytes[:, place * C : (place + 1) * C]

        def first_layer(unit):
            for e in unit:
                v[e] = psum_v.tile([P, H], F32, name="v_bank", tag="v")
                nc.tensor.matmul_mx(
                    out=v[e][:],
                    lhsT=x_slot[e].bitcast(FP8X4),
                    lhsT_scale=x_slot_plane[e],
                    rhs=w1[e].bitcast(packed(e)),
                    rhs_scale=s1[e],
                    start=True,
                    stop=True,
                )

        def rectify(unit):
            for e in unit:
                relu[e] = relu_ring.tile([P, PACK, P], F32, name="relu")
                src = v[e][:].rearrange("s (b a t) -> s b t a", a=4, t=PACK)
                dst = relu[e][:].rearrange("s t (b a) -> s b t a", a=4)
                if e in RELU_ON_SCALAR:
                    nc.scalar.activation(dst, src, ACT.Relu)
                else:
                    nc.vector.tensor_scalar(dst, src, 0.0, None, ALU.max)

        def turn(unit):
            for e in unit:
                turned[e] = psum_turned.tile([P, PACK, C], F32, name="turned_bank")
                for t in range(PACK):
                    nc.tensor.transpose(turned[e][:, t, :], relu[e][:, t, :], identity[:])

        def square(unit):
            h_bf[unit] = h_ring.tile([P, UNIT, C, PACK], BF16, name="h_bf", align_bytes=64)
            for place, e in enumerate(unit):
                nc.scalar.activation(h_bf[unit][:, place, :, :], turned[e][:].rearrange("m t s -> m s t"), ACT.Square)

        def quantise(unit):
            width = len(unit) * C
            h_words[unit] = codes.tile([P, UNIT * C], U32, name="h_words", align_bytes=64)
            h_plane[unit] = codes.tile([P, UNIT * C], U8, name="h_plane", align_bytes=64)
            nc.vector.quantize_mx(
                out=h_words[unit][:, :width].bitcast(FP8X4),
                scales=h_plane[unit][:, :width],
                in_=h_bf[unit][:].rearrange("m e s t -> m (e s t)")[:, : width * PACK],
            )

        def second_product(unit, half, bank):
            rows = slice(half * P, (half + 1) * P)
            for place, e in enumerate(unit):
                cols = slice(place * C, (place + 1) * C)
                nc.tensor.matmul_mx(
                    out=bank[:, cols],
                    lhsT=w2[e, half].bitcast(packed(e)),
                    lhsT_scale=s2[e][:, rows],
                    rhs=h_words[unit][:, cols].bitcast(FP8X4),
                    rhs_scale=h_plane[unit][:, cols],
                    start=True,
                    stop=True,
                )

        def second_layer(unit):
            y_bank[unit] = psum_y.tile([P, UNIT * C], F32, name="y_bank", tag="y")
            second_product(unit, 0, y_bank[unit][:])

        def keep_results(unit):
            dst = y[0][:, unit[0] * C : (unit[-1] + 1) * C]
            src = y_bank[unit][:, : len(unit) * C]
            if unit[0] in KEEP_ON_VECTOR:
                nc.vector.tensor_copy(dst, src)
            else:
                nc.scalar.copy(dst, src)

        leads = (
            (second_layer, -3),
            (gather_tokens, 1),
            (quantise, -2),
            (rectify, 0),
            (square, -1),
            (keep_results, -4),
            (first_layer, 1),
            (turn, 0),
        )
        with tc.psum_pool(name="psum_turned", bufs=3) as psum_turned:
            for j in range(-max(lead for stage, lead in leads), len(UNITS) - min(lead for stage, lead in leads)):
                for stage, lead in leads:
                    if 0 <= j + lead < len(UNITS):
                        stage(UNITS[j + lead])

        psum_late = ctx.enter_context(tc.psum_pool(name="psum_late", bufs=3))
        for one, other in zip(UNITS[0::2], UNITS[1::2]):
            bank = psum_late.tile([P, BANK], F32, name="late_bank", tag="late")
            second_product(one, 1, bank[:, : UNIT * C])
            second_product(other, 1, bank[:, UNIT * C :])
            nc.scalar.copy(y[1][:, one[0] * C : (other[-1] + 1) * C], bank[:, : (len(one) + len(other)) * C])

        def fetch_term(piece, r):
            half, first, end = piece
            term = keep.tile([P, end - first], F32, name="term_%d_%d_%d" % (half, first, r))
            listed = entries(pos_sb[r], first, end)
            nc.vector.tensor_tensor(term[:], y[half][:].indirect(listed), gate_sb[:, r, first:end], ALU.mult)
            return term

        for index, piece in enumerate(TENSOR_PIECES):
            half, first, end = piece
            blocks = (end - first) // P
            pool, tag = ((psum_v, "v"), (psum_late, "late"))[index % 2]
            sums = [pool.tile([P, BANK], F32, name="sum_bank", tag=tag) for b in range(blocks)]
            for r in range(TOP):
                term = fetch_term(piece, r)
                for b in range(blocks):
                    nc.tensor.matmul(
                        sums[b][:, :P],
                        lhsT=term[:, b * P : (b + 1) * P],
                        rhs=identity[:],
                        start=(r == 0),
                        stop=(r == TOP - 1),
                        is_transpose=True,
                    )
            by_token = keep.tile([P, blocks, P], F32, name="by_token_%d_%d" % (half, first))
            back = psum_y.tile([P, BANK], F32, name="back_bank", tag="y")
            for b in range(blocks):
                nc.scalar.copy(by_token[:, b, :], sums[b][:, :P])
                nc.tensor.transpose(back[:, b * P : (b + 1) * P], by_token[:, b, :], identity[:])
            result = keep.tile([P, end - first], F32, name="result_%d_%d" % (half, first))
            nc.scalar.copy(result[:], back[:, : end - first])
            nc.sync.dma_start(out=out[half * P : (half + 1) * P, first:end], in_=result[:])

        half, first, end = LAST_PIECE
        terms = [fetch_term(LAST_PIECE, r) for r in range(TOP)]
        middle = (end - first) // 2
        for r in range(1, TOP):
            for part in (slice(0, middle), slice(middle, end - first)):
                nc.vector.tensor_tensor(terms[0][:, part], terms[0][:, part], terms[r][:, part], ALU.add)
        nc.sync.dma_start(out=out[half * P : (half + 1) * P, first:end], in_=terms[0][:])
